import numpy as np
import ml_dtypes


def mxq(x, axis, fmt="e4m3"):
    dtype, down = {"e4m3": (ml_dtypes.float8_e4m3fn, 7), "e5m2": (ml_dtypes.float8_e5m2, 14)}[fmt]
    v = np.moveaxis(np.asarray(x, np.float32).astype(ml_dtypes.bfloat16).astype(np.float64), axis, -1)
    blocks = v.reshape(v.shape[:-1] + (-1, 32))
    amax = np.abs(blocks).max(-1, keepdims=True)
    byte = np.maximum(np.where(amax > 0, np.frexp(amax)[1] - 1 + 127, 0) - down, 1)
    scale = np.exp2(byte - 127.0)
    codes = (blocks / scale).astype(np.float32).astype(dtype).astype(np.float64)
    return np.moveaxis((codes * scale).reshape(v.shape), -1, axis)


WIDE = False


def mx_kscale(k):
    if not WIDE:
        return np.ones(k)
    levels = np.array([10, -10, 5, -5, 0])
    if k % 512:
        return np.exp2(np.random.permutation(np.resize(levels, k // 32))).repeat(32)
    a = np.empty((k // 512, 16))
    for p in range(k // 512):
        a[p, :8] = np.random.permutation(np.resize(levels, 8))
        for g in range(8):
            far = levels[np.abs(levels - a[p, g]) >= 10]
            a[p, g + 8] = far[np.random.randint(len(far))]
    return np.exp2(a.ravel()).repeat(32)


def f64(x):
    return np.asarray(x).astype(np.float64)


def striped(idx):
    return np.tile(idx.reshape(-1, 16).T, (8, 1)).astype(np.uint16)


def unstriped(offs):
    return offs[:16].T.reshape(-1).astype(np.int64)


def pack_weight(w):
    k, n = w.shape
    w = f64(np.asarray(w, np.float32).astype(ml_dtypes.bfloat16)).reshape(k // 32, 32, n)
    amax = np.abs(w).max(1)
    byte = np.clip(np.where(amax > 0, np.frexp(amax)[1] - 1 + 127 - 7, 1), 1, 254)
    scaled = (w * np.exp2(127.0 - byte)[:, None, :]).reshape(k, n).astype(np.float32)
    words = np.ascontiguousarray(scaled.reshape(k // 512, 128, 4, n).transpose(0, 1, 3, 2)).astype(ml_dtypes.float8_e4m3fn).view(np.uint8)
    return words, np.ascontiguousarray(byte.astype(np.uint8).reshape(k // 512, 16, n))


def unpack_weight(words, scales):
    g, p, n, _ = words.shape
    vals = np.ascontiguousarray(words).view(ml_dtypes.float8_e4m3fn).astype(np.float64) * np.repeat(np.exp2(scales.astype(np.float64) - 127.0), 8, axis=1)[..., None]
    return vals.transpose(0, 1, 3, 2).reshape(g * 512, n)


K, T, H, N = 512, 1024, 512, 128


def setup_inputs():
    n = np.random.standard_normal
    s = mx_kscale(K)[:, None]
    u = mx_kscale(H)
    packed_xT = pack_weight(n((K, T)) * s)
    packed_w2 = pack_weight(n((H, N)) / np.sqrt(3 * H) / u[:, None])
    packed_w3 = pack_weight(n((H, N)) / np.sqrt(3 * H) / u[:, None])
    packed_w4 = pack_weight(n((H, N)) / np.sqrt(3 * H) / u[:, None])
    return {
        "x_words": packed_xT[0],
        "x_scales": packed_xT[1],
        "w1": (n((K, H)) / np.sqrt(K) / s * u).astype(np.float32),
        "w2_words": packed_w2[0],
        "w2_scales": packed_w2[1],
        "w3_words": packed_w3[0],
        "w3_scales": packed_w3[1],
        "w4_words": packed_w4[0],
        "w4_scales": packed_w4[1],
        "pos1": striped(np.random.permutation(T)),
        "pos2": striped(np.random.permutation(T)),
        "pos3": striped(np.random.permutation(T)),
    }


def reference(x_words, x_scales, w1, w2_words, w2_scales, w3_words, w3_scales, w4_words, w4_scales, pos1, pos2, pos3):
    xq = unpack_weight(x_words, x_scales)
    h = mxq(f64(w1), 0, "e4m3").T @ xq
    g0 = h[:, unstriped(pos1)]
    g1 = h[:, unstriped(pos2)]
    g2 = h[:, unstriped(pos3)]
    z1 = (g0 + g1 + g2) / 3
    z2 = np.maximum(np.maximum(g0, g1), g2)
    z3 = np.minimum(np.minimum(g0, g1), g2)
    return unpack_weight(w2_words, w2_scales).T @ mxq(z1, 0, "e4m3") + unpack_weight(w3_words, w3_scales).T @ mxq(z2, 0, "e4m3") + unpack_weight(w4_words, w4_scales).T @ mxq(z3, 0, "e4m3")

@@ -1,0 +1,190 @@
+from contextlib import ExitStack
+
+import concourse.mybir as mybir
+from concourse.masks import make_identity
+
+K, T, H, N = 512, 1024, 512, 128
+FLOPS = 2 * K * H * T + 3 * 2 * H * N * T
+
+F32 = mybir.dt.float32
+BF16 = mybir.dt.bfloat16
+I32 = mybir.dt.int32
+U32 = mybir.dt.uint32
+U16 = mybir.dt.uint16
+U8 = mybir.dt.uint8
+FP8X4 = mybir.dt.float8_e4m3fn_x4
+MAX = mybir.AluOpType.max
+MIN = mybir.AluOpType.min
+COPY = mybir.ActivationFunctionType.Copy
+
+P = 128
+PACK = 4
+BANK = 512
+CHUNK = 512
+CHUNKS = T // CHUNK
+BLOCKS = CHUNK // P
+
+
+def tile_picked_wpna_none_l_kernel(
+    tc, x_words, x_scales, w1, w2_words, w2_scales, w3_words, w3_scales, w4_words, w4_scales, pos1, pos2, pos3, out
+):
+    nc = tc.nc
+    with ExitStack() as ctx:
+        keep = ctx.enter_context(tc.tile_pool(name="keep", bufs=1))
+        psum = ctx.enter_context(tc.psum_pool(name="psum", bufs=1))
+
+        def sb(name, shape, dtype):
+            return keep.tile(shape, dtype, name=name, align_bytes=64)
+
+        banks = [psum.tile([P, BANK], F32, name="bank%d" % b) for b in range(8)]
+
+        def load_scale_rows(queue, plane, rows):
+            for q in range(4):
+                queue.dma_start(out=plane[32 * q : 32 * q + 4, :].bitcast(I32), in_=rows[4 * q : 4 * q + 4, :].bitcast(I32))
+
+        x_plane = sb("x_plane", [P, T], U8)
+        nc.vector.memset(x_plane[:].bitcast(I32), 0)
+        w1_rows = w1.rearrange("(p j) c -> p j c", j=PACK)
+        half = H // 2
+        w1_raw = []
+        for a in range(2):
+            raw = sb("w1_raw%d" % a, [P, PACK, half], F32)
+            nc.sync.dma_start(out=raw[:], in_=w1_rows[:, :, a * half : (a + 1) * half])
+            w1_raw.append(raw)
+        load_scale_rows(nc.scalar, x_plane, x_scales[0])
+        x_flat = x_words[0].rearrange("p c r -> p (c r)")
+        x_codes = []
+        for u in range(2):
+            codes = sb("x_codes%d" % u, [P, BANK], U32)
+            nc.sync.dma_start(out=codes[:].bitcast(I32), in_=x_flat[:, u * BANK * PACK : (u + 1) * BANK * PACK].bitcast(I32))
+            x_codes.append(codes)
+        lists = []
+        for d, pos in enumerate((pos1, pos2, pos3)):
+            offsets = keep.tile([P, T // 16], U16, name="list%d" % d)
+            nc.sync.dma_start(offsets[:], pos)
+            lists.append(offsets)
+        wz_codes, wz_planes = [], []
+        for s, (words, scales) in enumerate(((w2_words, w2_scales), (w3_words, w3_scales), (w4_words, w4_scales))):
+            codes = sb("wz_codes%d" % s, [P, N], U32)
+            nc.sync.dma_start(out=codes[:].bitcast(I32), in_=words[0].rearrange("p c r -> p (c r)").bitcast(I32))
+            plane = sb("wz_plane%d" % s, [P, N], U8)
+            nc.vector.memset(plane[:].bitcast(I32), 0)
+            load_scale_rows(nc.sync, plane, scales[0])
+            wz_codes.append(codes)
+            wz_planes.append(plane)
+        identity = sb("identity", [P, P], F32)
+        make_identity(nc, identity[:])
+
+        w1_bf = [sb("w1_bf%d" % t, [P, P, PACK], BF16) for t in range(PACK)]
+        w1_codes = [sb("w1_codes%d" % t, [P, P], U32) for t in range(PACK)]
+        w1_planes = [sb("w1_plane%d" % t, [P, P], U8) for t in range(PACK)]
+        m_half = P // 2
+        for a in range(2):
+            dealt = w1_raw[a][:].rearrange("p j (m t) -> p t m j", t=PACK)
+            for t in range(PACK):
+                dst = w1_bf[t][:, a * m_half : (a + 1) * m_half, :]
+                if t < 2:
+                    nc.vector.tensor_copy(out=dst, in_=dealt[:, t])
+                else:
+                    nc.scalar.activation(out=dst, in_=dealt[:, t], func=COPY)
+        h = [sb("h%d" % t, [P, T], F32) for t in range(PACK)]
+        for t in range(PACK):
+            nc.vector.quantize_mx(
+                out=w1_codes[t][:].bitcast(FP8X4), scales=w1_planes[t][:], in_=w1_bf[t][:].rearrange("p m j -> p (m j)")
+            )
+            for u in range(2):
+                bank = banks[2 * t + u]
+                cols = slice(u * BANK, (u + 1) * BANK)
+                nc.tensor.matmul_mx(
+                    out=bank[:],
+                    lhsT=w1_codes[t][:].bitcast(FP8X4),
+                    lhsT_scale=w1_planes[t][:],
+                    rhs=x_codes[u][:].bitcast(FP8X4),
+                    rhs_scale=x_plane[:, cols],
+                    start=True,
+                    stop=True,
+                )
+                if (t, u) == (0, 1):
+                    nc.vector.tensor_copy(out=h[t][:, cols], in_=bank[:])
+                else:
+                    nc.scalar.copy(out=h[t][:, cols], in_=bank[:])
+
+        picked = [[sb("picked%d_%d" % (c, d), [P, PACK, CHUNK], F32) for d in range(3)] for c in range(CHUNKS)]
+        for c in range(CHUNKS):
+            for d in range(3):
+                offsets = lists[d][:, c * CHUNK // 16 : (c + 1) * CHUNK // 16]
+                for t in range(PACK):
+                    nc.vector.tensor_copy(out=picked[c][d][:, t, :], in_=h[t][:].indirect(offsets))
+
+        rounded = [[sb("rounded%d_%d" % (c, d), [P, CHUNK, PACK], BF16) for d in range(3)] for c in range(CHUNKS)]
+        mean = [sb("mean%d" % c, [P, CHUNK, PACK], BF16) for c in range(CHUNKS)]
+        for c in range(CHUNKS):
+            for d in range(3):
+                nc.scalar.activation(out=rounded[c][d][:], in_=picked[c][d][:].rearrange("p t v -> p v t"), func=COPY)
+            for t in range(PACK):
+                for b in range(BLOCKS):
+                    for d in range(3):
+                        nc.tensor.matmul(
+                            banks[b][:, t * P : (t + 1) * P],
+                            picked[c][d][:, t, b * P : (b + 1) * P],
+                            identity[:],
+                            start=(d == 0),
+                            stop=(d == 2),
+                            is_transpose=True,
+                        )
+            for pair in range(BLOCKS // 2):
+                back = banks[4 + 2 * c + pair]
+                back_view = back[:].rearrange("p (u v) -> p u v", u=2)
+                for e in range(2):
+                    b = 2 * pair + e
+                    turned = sb("turned%d_%d" % (c, b), [P, 2, P, 2], BF16)
+                    nc.scalar.activation(
+                        out=turned[:],
+                        in_=banks[b][:].rearrange("v (u e p) -> v u p e", u=2, e=2),
+                        func=COPY,
+                        scale=1.0 / 3.0,
+                    )
+                    words = turned[:].rearrange("v u p e -> v (u p e)").bitcast(F32)
+                    for u in range(2):
+                        nc.tensor.transpose(back_view[:, u, e * P : (e + 1) * P], words[:, u * P : (u + 1) * P], identity[:])
+                dst = mean[c][:, pair * 2 * P : (pair + 1) * 2 * P, :].rearrange("p v t -> p (v t)").bitcast(F32)
+                nc.scalar.copy(out=dst.rearrange("p (v u) -> p v u", u=2), in_=back[:].rearrange("p (u v) -> p v u", u=2))
+
+        pieces = [[(0, CHUNK, banks[7])], [(0, CHUNK // 2, banks[6]), (CHUNK // 2, CHUNK, banks[5])]]
+        for c in range(CHUNKS):
+            flat = [r[:].rearrange("p v t -> p (v t)") for r in rounded[c]]
+            stats = [mean[c][:].rearrange("p v t -> p (v t)")]
+            first = []
+            for name, op in (("max", MAX), ("min", MIN)):
+                two = sb("%s2_%d" % (name, c), [P, CHUNK * PACK], BF16)
+                nc.vector.tensor_tensor(two[:], flat[0], flat[1], op)
+                first.append(two)
+            for (name, op), two in zip((("max", MAX), ("min", MIN)), first):
+                three = sb("%s3_%d" % (name, c), [P, CHUNK * PACK], BF16)
+                nc.vector.tensor_tensor(three[:], two[:], flat[2], op)
+                stats.append(three[:])
+            for s in range(3):
+                codes = sb("z_codes%d_%d" % (c, s), [P, CHUNK], U32)
+                plane = sb("z_plane%d_%d" % (c, s), [P, CHUNK], U8)
+                spans = [(lo, hi) for lo, hi, bank in pieces[c]] if s == 2 else [(0, CHUNK)]
+                for lo, hi in spans:
+                    nc.vector.quantize_mx(
+                        out=codes[:, lo:hi].bitcast(FP8X4), scales=plane[:, lo:hi], in_=stats[s][:, lo * PACK : hi * PACK]
+                    )
+                for lo, hi, bank in pieces[c]:
+                    nc.tensor.matmul_mx(
+                        out=bank[:, : hi - lo],
+                        lhsT=wz_codes[s][:].bitcast(FP8X4),
+                        lhsT_scale=wz_planes[s][:],
+                        rhs=codes[:, lo:hi].bitcast(FP8X4),
+                        rhs_scale=plane[:, lo:hi],
+                        start=(s == 0),
+                        stop=(s == 2),
+                    )
+            for i, (lo, hi, bank) in enumerate(pieces[c]):
+                result = sb("result%d_%d" % (c, i), [P, hi - lo], F32)
+                if (c, i) == (CHUNKS - 1, 1):
+                    nc.vector.tensor_copy(out=result[:], in_=bank[:, : hi - lo])
+                else:
+                    nc.scalar.copy(out=result[:], in_=bank[:, : hi - lo])
+                nc.sync.dma_start(out=out[:, c * CHUNK + lo : c * CHUNK + hi], in_=result[:])

@@ -43,7 +43,7 @@ def tile_picked_wpna_none_l_kernel(
                 queue.dma_start(out=plane[32 * q : 32 * q + 4, :].bitcast(I32), in_=rows[4 * q : 4 * q + 4, :].bitcast(I32))
 
         x_plane = sb("x_plane", [P, T], U8)
-        nc.vector.memset(x_plane[:].bitcast(I32), 0)
+        nc.gpsimd.memset(x_plane[:].bitcast(I32), 0)
         w1_rows = w1.rearrange("(p j) c -> p j c", j=PACK)
         half = H // 2
         w1_raw = []
@@ -64,11 +64,11 @@ def tile_picked_wpna_none_l_kernel(
             nc.sync.dma_start(offsets[:], pos)
             lists.append(offsets)
         wz_codes, wz_planes = [], []
-        for s, (words, scales) in enumerate(((w2_words, w2_scales), (w3_words, w3_scales), (w4_words, w4_scales))):
+        for s, (words, scales) in enumerate(((w3_words, w3_scales), (w4_words, w4_scales), (w2_words, w2_scales))):
             codes = sb("wz_codes%d" % s, [P, N], U32)
             nc.sync.dma_start(out=codes[:].bitcast(I32), in_=words[0].rearrange("p c r -> p (c r)").bitcast(I32))
             plane = sb("wz_plane%d" % s, [P, N], U8)
-            nc.vector.memset(plane[:].bitcast(I32), 0)
+            nc.gpsimd.memset(plane[:].bitcast(I32), 0)
             load_scale_rows(nc.sync, plane, scales[0])
             wz_codes.append(codes)
             wz_planes.append(plane)
@@ -87,34 +87,37 @@ def tile_picked_wpna_none_l_kernel(
                     nc.vector.tensor_copy(out=dst, in_=dealt[:, t])
                 else:
                     nc.scalar.activation(out=dst, in_=dealt[:, t], func=COPY)
-        h = [sb("h%d" % t, [P, T], F32) for t in range(PACK)]
+        h = sb("h", [P, PACK * T], F32)
         for t in range(PACK):
             nc.vector.quantize_mx(
                 out=w1_codes[t][:].bitcast(FP8X4), scales=w1_planes[t][:], in_=w1_bf[t][:].rearrange("p m j -> p (m j)")
             )
-            for u in range(2):
-                bank = banks[2 * t + u]
-                cols = slice(u * BANK, (u + 1) * BANK)
+            width = BANK // 2 if t == 0 else BANK
+            for i, lo in enumerate(range(0, T, width)):
+                bank = banks[i if t == 0 else (2 * t + 2 + i) % 8]
+                u, inner = divmod(lo, BANK)
                 nc.tensor.matmul_mx(
-                    out=bank[:],
+                    out=bank[:, :width],
                     lhsT=w1_codes[t][:].bitcast(FP8X4),
                     lhsT_scale=w1_planes[t][:],
-                    rhs=x_codes[u][:].bitcast(FP8X4),
-                    rhs_scale=x_plane[:, cols],
+                    rhs=x_codes[u][:, inner : inner + width].bitcast(FP8X4),
+                    rhs_scale=x_plane[:, lo : lo + width],
                     start=True,
                     stop=True,
                 )
-                if (t, u) == (0, 1):
-                    nc.vector.tensor_copy(out=h[t][:, cols], in_=bank[:])
+                dst = h[:, t * T + lo : t * T + lo + width]
+                if t == 0 and i % 2 == 1:
+                    nc.vector.tensor_copy(out=dst, in_=bank[:, :width])
                 else:
-                    nc.scalar.copy(out=h[t][:, cols], in_=bank[:])
+                    nc.scalar.copy(out=dst, in_=bank[:, :width])
 
         picked = [[sb("picked%d_%d" % (c, d), [P, PACK, CHUNK], F32) for d in range(3)] for c in range(CHUNKS)]
         for c in range(CHUNKS):
             for d in range(3):
                 offsets = lists[d][:, c * CHUNK // 16 : (c + 1) * CHUNK // 16]
                 for t in range(PACK):
-                    nc.vector.tensor_copy(out=picked[c][d][:, t, :], in_=h[t][:].indirect(offsets))
+                    end = (t + 1) * T if (c, d) == (0, 0) else PACK * T
+                    nc.vector.tensor_copy(out=picked[c][d][:, t, :], in_=h[:, t * T : end].indirect(offsets))
 
         rounded = [[sb("rounded%d_%d" % (c, d), [P, CHUNK, PACK], BF16) for d in range(3)] for c in range(CHUNKS)]
         mean = [sb("mean%d" % c, [P, CHUNK, PACK], BF16) for c in range(CHUNKS)]
@@ -150,10 +153,10 @@ def tile_picked_wpna_none_l_kernel(
                 dst = mean[c][:, pair * 2 * P : (pair + 1) * 2 * P, :].rearrange("p v t -> p (v t)").bitcast(F32)
                 nc.scalar.copy(out=dst.rearrange("p (v u) -> p v u", u=2), in_=back[:].rearrange("p (u v) -> p v u", u=2))
 
-        pieces = [[(0, CHUNK, banks[7])], [(0, CHUNK // 2, banks[6]), (CHUNK // 2, CHUNK, banks[5])]]
+        pieces = [[(0, CHUNK, banks[3])], [(0, CHUNK // 2, banks[7]), (CHUNK // 2, CHUNK, banks[3])]]
         for c in range(CHUNKS):
             flat = [r[:].rearrange("p v t -> p (v t)") for r in rounded[c]]
-            stats = [mean[c][:].rearrange("p v t -> p (v t)")]
+            stats = []
             first = []
             for name, op in (("max", MAX), ("min", MIN)):
                 two = sb("%s2_%d" % (name, c), [P, CHUNK * PACK], BF16)
@@ -163,6 +166,7 @@ def tile_picked_wpna_none_l_kernel(
                 three = sb("%s3_%d" % (name, c), [P, CHUNK * PACK], BF16)
                 nc.vector.tensor_tensor(three[:], two[:], flat[2], op)
                 stats.append(three[:])
+            stats.append(mean[c][:].rearrange("p v t -> p (v t)"))
             for s in range(3):
                 codes = sb("z_codes%d_%d" % (c, s), [P, CHUNK], U32)
                 plane = sb("z_plane%d_%d" % (c, s), [P, CHUNK], U8)

@@ -15,6 +15,10 @@ U8 = mybir.dt.uint8
 FP8X4 = mybir.dt.float8_e4m3fn_x4
 MAX = mybir.AluOpType.max
 MIN = mybir.AluOpType.min
+ADD = mybir.AluOpType.add
+SUB = mybir.AluOpType.subtract
+F32_MAX = 3.4028234663852886e38
+GROUP = 256
 COPY = mybir.ActivationFunctionType.Copy
 
 P = 128
@@ -111,28 +115,63 @@ def tile_picked_wpna_none_l_kernel(
                 else:
                     nc.scalar.copy(out=dst, in_=bank[:, :width])
 
-        picked = [[sb("picked%d_%d" % (c, d), [P, PACK, CHUNK], F32) for d in range(3)] for c in range(CHUNKS)]
-        for c in range(CHUNKS):
-            for d in range(3):
-                offsets = lists[d][:, c * CHUNK // 16 : (c + 1) * CHUNK // 16]
-                for t in range(PACK):
-                    end = (t + 1) * T if (c, d) == (0, 0) else PACK * T
-                    nc.vector.tensor_copy(out=picked[c][d][:, t, :], in_=h[:, t * T : end].indirect(offsets))
+        def shared(name, shape, dtype, tag):
+            return keep.tile(shape, dtype, name=name, tag=tag, align_bytes=64)
 
-        rounded = [[sb("rounded%d_%d" % (c, d), [P, CHUNK, PACK], BF16) for d in range(3)] for c in range(CHUNKS)]
+        def gather(dst, t, d, lo, hi, planes):
+            end = min(t + planes, PACK) * T
+            nc.vector.tensor_copy(out=dst, in_=h[:, t * T : end].indirect(lists[d][:, lo // 16 : hi // 16]))
+
+        def flat(ap):
+            return ap.rearrange("p t v -> p (t v)")
+
+        early = [[sb("early%d_%d" % (g, d), [P, PACK, GROUP], F32) for d in range(2)] for g in range(2)]
+        for t in range(PACK):
+            for d in range(2):
+                gather(early[0][d][:, t, :], t, d, 0, GROUP, 1)
+        for t in range(PACK):
+            for d in range(2):
+                gather(early[1][d][:, t, :], t, d, GROUP, CHUNK, 2)
+        third0 = sb("third0", [P, PACK, CHUNK], F32)
+        for t in range(PACK):
+            gather(third0[:, t, :], t, 2, 0, CHUNK, PACK)
+        late = [sb("late%d" % d, [P, PACK, CHUNK], F32) for d in range(2)]
+        for d in range(2):
+            for t in range(PACK):
+                gather(late[d][:, t, :], t, d, CHUNK, T, PACK)
+
+        def larger_smaller(a, b, diff, excess, larger, smaller):
+            nc.gpsimd.tensor_tensor(flat(diff), flat(a), flat(b), SUB)
+            nc.gpsimd.tensor_scalar(flat(excess), flat(diff), F32_MAX, 0.0, MIN, MAX)
+            nc.gpsimd.tensor_tensor(flat(larger), flat(b), flat(excess), ADD)
+            nc.gpsimd.tensor_tensor(flat(smaller), flat(a), flat(excess), SUB)
+
+        larger0 = shared("larger0", [P, PACK, GROUP], F32, "larger0")
+        smaller0 = shared("smaller0", [P, PACK, GROUP], F32, "smaller0")
+        for i in range(2):
+            planes = slice(2 * i, 2 * i + 2)
+            diff = shared("diff0_%d" % i, [P, 2, GROUP], F32, "excess0_%d" % (i - 1))
+            excess = shared("excess0_%d" % i, [P, 2, GROUP], F32, "excess0_%d" % i)
+            larger_smaller(
+                early[0][0][:, planes, :], early[0][1][:, planes, :], diff[:], excess[:], larger0[:, planes, :], smaller0[:, planes, :]
+            )
+        diff1 = shared("diff1", [P, PACK, GROUP], F32, "excess0_1")
+        excess1 = sb("excess1", [P, PACK, GROUP], F32)
+        pair1 = shared("pair1", [P, 2, PACK, GROUP], F32, "pair1")
+        larger_smaller(early[1][0][:], early[1][1][:], diff1[:], excess1[:], pair1[:, 0], pair1[:, 1])
+
         mean = [sb("mean%d" % c, [P, CHUNK, PACK], BF16) for c in range(CHUNKS)]
-        for c in range(CHUNKS):
-            for d in range(3):
-                nc.scalar.activation(out=rounded[c][d][:], in_=picked[c][d][:].rearrange("p t v -> p v t"), func=COPY)
+
+        def make_mean(c, source, turned):
             for t in range(PACK):
                 for b in range(BLOCKS):
-                    for d in range(3):
+                    for d in (2, 1, 0):
                         nc.tensor.matmul(
                             banks[b][:, t * P : (t + 1) * P],
-                            picked[c][d][:, t, b * P : (b + 1) * P],
+                            source(d, t, b),
                             identity[:],
-                            start=(d == 0),
-                            stop=(d == 2),
+                            start=(d == 2),
+                            stop=(d == 0),
                             is_transpose=True,
                         )
             for pair in range(BLOCKS // 2):
@@ -140,31 +179,64 @@ def tile_picked_wpna_none_l_kernel(
                 back_view = back[:].rearrange("p (u v) -> p u v", u=2)
                 for e in range(2):
                     b = 2 * pair + e
-                    turned = sb("turned%d_%d" % (c, b), [P, 2, P, 2], BF16)
                     nc.scalar.activation(
-                        out=turned[:],
+                        out=turned[b].rearrange("v (u p e) -> v u p e", u=2, e=2),
                         in_=banks[b][:].rearrange("v (u e p) -> v u p e", u=2, e=2),
                         func=COPY,
                         scale=1.0 / 3.0,
                     )
-                    words = turned[:].rearrange("v u p e -> v (u p e)").bitcast(F32)
+                    words = turned[b].bitcast(F32)
                     for u in range(2):
                         nc.tensor.transpose(back_view[:, u, e * P : (e + 1) * P], words[:, u * P : (u + 1) * P], identity[:])
                 dst = mean[c][:, pair * 2 * P : (pair + 1) * 2 * P, :].rearrange("p v t -> p (v t)").bitcast(F32)
                 nc.scalar.copy(out=dst.rearrange("p (v u) -> p v u", u=2), in_=back[:].rearrange("p (u v) -> p v u", u=2))
 
+        def round_planes(dst, src):
+            nc.scalar.activation(out=dst.rearrange("p (v t) -> p v t", t=PACK), in_=src.rearrange("p t v -> p v t"), func=COPY)
+
+        W = CHUNK * PACK
+        two0 = sb("two0", [P, 2, CHUNK, PACK], BF16)
+
+        for s, src in enumerate((larger0, smaller0)):
+            nc.scalar.activation(out=two0[:, s, :GROUP, :], in_=src[:].rearrange("p t v -> p v t"), func=COPY)
+        rounded_third0 = shared("rounded_third0", [P, W], BF16, "larger0")
+        round_planes(rounded_third0[:], third0[:])
+        turned0 = shared("turned0", [P, W], BF16, "smaller0")
+
+        def source0(d, t, b):
+            if d == 2:
+                return third0[:, t, b * P : (b + 1) * P]
+            g, inner = divmod(b * P, GROUP)
+            return early[g][d][:, t, inner : inner + P]
+
+        make_mean(0, source0, [turned0[:, b * H : (b + 1) * H] for b in range(BLOCKS)])
+        nc.scalar.activation(out=two0[:, :, GROUP:, :], in_=pair1[:].rearrange("p s t v -> p s v t"), func=COPY)
+        third1 = shared("third1", [P, PACK, CHUNK], F32, "smaller0")
+        for t in range(PACK):
+            gather(third1[:, t, :], t, 2, CHUNK, T, PACK)
+        late.append(third1)
+        rounded1 = shared("rounded1", [P, 3 * W], BF16, "pair1")
+        for d in range(3):
+            round_planes(rounded1[:, d * W : (d + 1) * W], late[d][:])
+        turned1 = [sb("turned1_%d" % b, [P, H], BF16) for b in range(BLOCKS)]
+        make_mean(1, lambda d, t, b: late[d][:, t, b * P : (b + 1) * P], [x[:] for x in turned1])
+
         pieces = [[(0, CHUNK, banks[3])], [(0, CHUNK // 2, banks[7]), (CHUNK // 2, CHUNK, banks[3])]]
         for c in range(CHUNKS):
-            flat = [r[:].rearrange("p v t -> p (v t)") for r in rounded[c]]
             stats = []
-            first = []
-            for name, op in (("max", MAX), ("min", MIN)):
-                two = sb("%s2_%d" % (name, c), [P, CHUNK * PACK], BF16)
-                nc.vector.tensor_tensor(two[:], flat[0], flat[1], op)
-                first.append(two)
+            if c == 0:
+                first = [two0[:, s].rearrange("p v t -> p (v t)") for s in range(2)]
+                last = rounded_third0[:]
+            else:
+                first = []
+                last = rounded1[:, 2 * W :]
+                for name, op in (("max", MAX), ("min", MIN)):
+                    two = sb("%s2_%d" % (name, c), [P, W], BF16)
+                    nc.vector.tensor_tensor(two[:], rounded1[:, :W], rounded1[:, W : 2 * W], op)
+                    first.append(two[:])
             for (name, op), two in zip((("max", MAX), ("min", MIN)), first):
-                three = sb("%s3_%d" % (name, c), [P, CHUNK * PACK], BF16)
-                nc.vector.tensor_tensor(three[:], two[:], flat[2], op)
+                three = sb("%s3_%d" % (name, c), [P, W], BF16)
+                nc.vector.tensor_tensor(three[:], two, last, op)
                 stats.append(three[:])
             stats.append(mean[c][:].rearrange("p v t -> p (v t)"))
             for s in range(3):

@@ -17,9 +17,8 @@ MAX = mybir.AluOpType.max
 MIN = mybir.AluOpType.min
 ADD = mybir.AluOpType.add
 SUB = mybir.AluOpType.subtract
-F32_MAX = 3.4028234663852886e38
-GROUP = 256
 COPY = mybir.ActivationFunctionType.Copy
+F32_MAX = 3.4028234663852886e38
 
 P = 128
 PACK = 4
@@ -27,6 +26,9 @@ BANK = 512
 CHUNK = 512
 CHUNKS = T // CHUNK
 BLOCKS = CHUNK // P
+GROUP = CHUNK // 2
+WOVEN = CHUNK * PACK
+PER_COLUMN = 16
 
 
 def tile_picked_wpna_none_l_kernel(
@@ -37,75 +39,91 @@ def tile_picked_wpna_none_l_kernel(
         keep = ctx.enter_context(tc.tile_pool(name="keep", bufs=1))
         psum = ctx.enter_context(tc.psum_pool(name="psum", bufs=1))
 
-        def sb(name, shape, dtype):
+        def own(name, shape, dtype):
             return keep.tile(shape, dtype, name=name, align_bytes=64)
+
+        def shared(name, shape, dtype, tag):
+            return keep.tile(shape, dtype, name=name, tag=tag, align_bytes=64)
 
         banks = [psum.tile([P, BANK], F32, name="bank%d" % b) for b in range(8)]
 
-        def load_scale_rows(queue, plane, rows):
+        def load_scale_rows(queue, scale_tile, rows):
             for q in range(4):
-                queue.dma_start(out=plane[32 * q : 32 * q + 4, :].bitcast(I32), in_=rows[4 * q : 4 * q + 4, :].bitcast(I32))
+                queue.dma_start(
+                    out=scale_tile[32 * q : 32 * q + 4, :].bitcast(I32), in_=rows[4 * q : 4 * q + 4, :].bitcast(I32)
+                )
 
-        x_plane = sb("x_plane", [P, T], U8)
-        nc.gpsimd.memset(x_plane[:].bitcast(I32), 0)
+        x_scale_tile = own("x_scale_tile", [P, T], U8)
+        nc.gpsimd.memset(x_scale_tile[:].bitcast(I32), 0)
         w1_rows = w1.rearrange("(p j) c -> p j c", j=PACK)
-        half = H // 2
+        half_h = H // 2
         w1_raw = []
         for a in range(2):
-            raw = sb("w1_raw%d" % a, [P, PACK, half], F32)
-            nc.sync.dma_start(out=raw[:], in_=w1_rows[:, :, a * half : (a + 1) * half])
+            raw = own("w1_raw%d" % a, [P, PACK, half_h], F32)
+            nc.sync.dma_start(out=raw[:], in_=w1_rows[:, :, a * half_h : (a + 1) * half_h])
             w1_raw.append(raw)
-        load_scale_rows(nc.scalar, x_plane, x_scales[0])
+        load_scale_rows(nc.scalar, x_scale_tile, x_scales[0])
         x_flat = x_words[0].rearrange("p c r -> p (c r)")
         x_codes = []
-        for u in range(2):
-            codes = sb("x_codes%d" % u, [P, BANK], U32)
+        for u in range(T // BANK):
+            codes = own("x_codes%d" % u, [P, BANK], U32)
             nc.sync.dma_start(out=codes[:].bitcast(I32), in_=x_flat[:, u * BANK * PACK : (u + 1) * BANK * PACK].bitcast(I32))
             x_codes.append(codes)
         lists = []
         for d, pos in enumerate((pos1, pos2, pos3)):
-            offsets = keep.tile([P, T // 16], U16, name="list%d" % d)
+            offsets = keep.tile([P, T // PER_COLUMN], U16, name="list%d" % d)
             nc.sync.dma_start(offsets[:], pos)
             lists.append(offsets)
-        wz_codes, wz_planes = [], []
+        wz_codes, wz_scale_tiles = [], []
         for s, (words, scales) in enumerate(((w3_words, w3_scales), (w4_words, w4_scales), (w2_words, w2_scales))):
-            codes = sb("wz_codes%d" % s, [P, N], U32)
+            codes = own("wz_codes%d" % s, [P, N], U32)
             nc.sync.dma_start(out=codes[:].bitcast(I32), in_=words[0].rearrange("p c r -> p (c r)").bitcast(I32))
-            plane = sb("wz_plane%d" % s, [P, N], U8)
-            nc.gpsimd.memset(plane[:].bitcast(I32), 0)
-            load_scale_rows(nc.sync, plane, scales[0])
+            scale_tile = own("wz_scale_tile%d" % s, [P, N], U8)
+            nc.gpsimd.memset(scale_tile[:].bitcast(I32), 0)
+            load_scale_rows(nc.sync, scale_tile, scales[0])
             wz_codes.append(codes)
-            wz_planes.append(plane)
-        identity = sb("identity", [P, P], F32)
+            wz_scale_tiles.append(scale_tile)
+        identity = own("identity", [P, P], F32)
         make_identity(nc, identity[:])
 
-        w1_bf = [sb("w1_bf%d" % t, [P, P, PACK], BF16) for t in range(PACK)]
-        w1_codes = [sb("w1_codes%d" % t, [P, P], U32) for t in range(PACK)]
-        w1_planes = [sb("w1_plane%d" % t, [P, P], U8) for t in range(PACK)]
-        m_half = P // 2
-        for a in range(2):
-            dealt = w1_raw[a][:].rearrange("p j (m t) -> p t m j", t=PACK)
-            for t in range(PACK):
-                dst = w1_bf[t][:, a * m_half : (a + 1) * m_half, :]
-                if t < 2:
-                    nc.vector.tensor_copy(out=dst, in_=dealt[:, t])
-                else:
-                    nc.scalar.activation(out=dst, in_=dealt[:, t], func=COPY)
-        h = sb("h", [P, PACK * T], F32)
-        for t in range(PACK):
+        sets = ((0, 1), (1, 2), (2, 4))
+        w1_bf = [own("w1_bf%d" % lo, [P, hi - lo, P, PACK], BF16) for lo, hi in sets]
+        w1_codes = [own("w1_codes%d" % lo, [P, (hi - lo) * P], U32) for lo, hi in sets]
+        w1_scale_tiles = [own("w1_scale_tile%d" % lo, [P, (hi - lo) * P], U8) for lo, hi in sets]
+        half_m = P // 2
+        dealt = [raw[:].rearrange("p j (m t) -> p t m j", t=PACK) for raw in w1_raw]
+
+        def w1_part(s, a, lo, hi):
+            return w1_bf[s][:, :, a * half_m + lo : a * half_m + hi, :], dealt[a][:, sets[s][0] : sets[s][1], lo:hi, :]
+
+        nc.vector.tensor_copy(*w1_part(0, 0, 0, half_m))
+        nc.vector.tensor_copy(*w1_part(1, 0, 0, half_m))
+        nc.scalar.activation(*w1_part(2, 0, 0, half_m), func=COPY)
+        nc.vector.tensor_copy(*w1_part(0, 1, 0, half_m // 2))
+        nc.scalar.activation(*w1_part(0, 1, half_m // 2, half_m), func=COPY)
+        nc.scalar.activation(*w1_part(1, 1, 0, half_m), func=COPY)
+        nc.scalar.activation(*w1_part(2, 1, 0, half_m), func=COPY)
+        for s in range(len(sets)):
             nc.vector.quantize_mx(
-                out=w1_codes[t][:].bitcast(FP8X4), scales=w1_planes[t][:], in_=w1_bf[t][:].rearrange("p m j -> p (m j)")
+                out=w1_codes[s][:].bitcast(FP8X4),
+                scales=w1_scale_tiles[s][:],
+                in_=w1_bf[s][:].rearrange("p t m j -> p (t m j)"),
             )
+
+        h = own("h", [P, PACK * T], F32)
+        for t in range(PACK):
+            s = min(t, len(sets) - 1)
+            m_cols = slice((t - s) * P, (t - s + 1) * P)
             width = BANK // 2 if t == 0 else BANK
             for i, lo in enumerate(range(0, T, width)):
-                bank = banks[i if t == 0 else (2 * t + 2 + i) % 8]
+                bank = banks[i if t == 0 else 2 * (t - 1) + i]
                 u, inner = divmod(lo, BANK)
                 nc.tensor.matmul_mx(
                     out=bank[:, :width],
-                    lhsT=w1_codes[t][:].bitcast(FP8X4),
-                    lhsT_scale=w1_planes[t][:],
+                    lhsT=w1_codes[s][:, m_cols].bitcast(FP8X4),
+                    lhsT_scale=w1_scale_tiles[s][:, m_cols],
                     rhs=x_codes[u][:, inner : inner + width].bitcast(FP8X4),
-                    rhs_scale=x_plane[:, lo : lo + width],
+                    rhs_scale=x_scale_tile[:, lo : lo + width],
                     start=True,
                     stop=True,
                 )
@@ -115,52 +133,50 @@ def tile_picked_wpna_none_l_kernel(
                 else:
                     nc.scalar.copy(out=dst, in_=bank[:, :width])
 
-        def shared(name, shape, dtype, tag):
-            return keep.tile(shape, dtype, name=name, tag=tag, align_bytes=64)
+        def gather(dst, t, d, lo, hi, span):
+            end = min(t + span, PACK) * T
+            offsets = lists[d][:, lo // PER_COLUMN : hi // PER_COLUMN]
+            nc.vector.tensor_copy(out=dst, in_=h[:, t * T : end].indirect(offsets))
 
-        def gather(dst, t, d, lo, hi, planes):
-            end = min(t + planes, PACK) * T
-            nc.vector.tensor_copy(out=dst, in_=h[:, t * T : end].indirect(lists[d][:, lo // 16 : hi // 16]))
-
-        def flat(ap):
-            return ap.rearrange("p t v -> p (t v)")
-
-        early = [[sb("early%d_%d" % (g, d), [P, PACK, GROUP], F32) for d in range(2)] for g in range(2)]
-        for t in range(PACK):
-            for d in range(2):
-                gather(early[0][d][:, t, :], t, d, 0, GROUP, 1)
-        for t in range(PACK):
-            for d in range(2):
-                gather(early[1][d][:, t, :], t, d, GROUP, CHUNK, 2)
-        third0 = sb("third0", [P, PACK, CHUNK], F32)
+        plane0 = [own("plane0_%d" % d, [P, CHUNK], F32) for d in range(2)]
+        rest = [[own("rest%d_%d" % (g, d), [P, (PACK - 1) * GROUP], F32) for d in range(2)] for g in range(2)]
+        for d in range(2):
+            gather(plane0[d][:], 0, d, 0, CHUNK, 1)
+        for g in range(2):
+            for t in range(1, PACK):
+                for d in range(2):
+                    gather(rest[g][d][:, (t - 1) * GROUP : t * GROUP], t, d, g * GROUP, (g + 1) * GROUP, 1 + g)
+        third0 = own("third0", [P, PACK, CHUNK], F32)
         for t in range(PACK):
             gather(third0[:, t, :], t, 2, 0, CHUNK, PACK)
-        late = [sb("late%d" % d, [P, PACK, CHUNK], F32) for d in range(2)]
+        picked1 = [own("picked1_%d" % d, [P, PACK, CHUNK], F32) for d in range(2)]
         for d in range(2):
             for t in range(PACK):
-                gather(late[d][:, t, :], t, d, CHUNK, T, PACK)
+                gather(picked1[d][:, t, :], t, d, CHUNK, T, PACK)
 
-        def larger_smaller(a, b, diff, excess, larger, smaller):
-            nc.gpsimd.tensor_tensor(flat(diff), flat(a), flat(b), SUB)
-            nc.gpsimd.tensor_scalar(flat(excess), flat(diff), F32_MAX, 0.0, MIN, MAX)
-            nc.gpsimd.tensor_tensor(flat(larger), flat(b), flat(excess), ADD)
-            nc.gpsimd.tensor_tensor(flat(smaller), flat(a), flat(excess), SUB)
+        group_cols = PACK * GROUP
+        larger0 = shared("larger0", [P, group_cols], F32, "larger0")
+        smaller0 = shared("smaller0", [P, group_cols], F32, "smaller0")
+        both1 = shared("both1", [P, 2 * group_cols], F32, "both1")
+        extremes = ((larger0[:], smaller0[:]), (both1[:, :group_cols], both1[:, group_cols:]))
+        diff = own("diff_plane0", [P, CHUNK], F32)
+        excess = shared("excess_plane0", [P, CHUNK], F32, "excess0")
+        nc.gpsimd.tensor_tensor(diff[:], plane0[0][:], plane0[1][:], SUB)
+        nc.gpsimd.tensor_scalar(excess[:], diff[:], F32_MAX, 0.0, MIN, MAX)
+        for g, (larger, smaller) in enumerate(extremes):
+            cols = slice(g * GROUP, (g + 1) * GROUP)
+            nc.gpsimd.tensor_tensor(larger[:, :GROUP], plane0[1][:, cols], excess[:, cols], ADD)
+            nc.gpsimd.tensor_tensor(smaller[:, :GROUP], plane0[0][:, cols], excess[:, cols], SUB)
+        for g, (larger, smaller) in enumerate(extremes):
+            a, b = rest[g]
+            diff = shared("diff_rest%d" % g, [P, group_cols - GROUP], F32, "excess%d" % g)
+            excess = shared("excess_rest%d" % g, [P, group_cols - GROUP], F32, "excess%d" % (g + 1))
+            nc.gpsimd.tensor_tensor(diff[:], a[:], b[:], SUB)
+            nc.gpsimd.tensor_scalar(excess[:], diff[:], F32_MAX, 0.0, MIN, MAX)
+            nc.gpsimd.tensor_tensor(larger[:, GROUP:], b[:], excess[:], ADD)
+            nc.gpsimd.tensor_tensor(smaller[:, GROUP:], a[:], excess[:], SUB)
 
-        larger0 = shared("larger0", [P, PACK, GROUP], F32, "larger0")
-        smaller0 = shared("smaller0", [P, PACK, GROUP], F32, "smaller0")
-        for i in range(2):
-            planes = slice(2 * i, 2 * i + 2)
-            diff = shared("diff0_%d" % i, [P, 2, GROUP], F32, "excess0_%d" % (i - 1))
-            excess = shared("excess0_%d" % i, [P, 2, GROUP], F32, "excess0_%d" % i)
-            larger_smaller(
-                early[0][0][:, planes, :], early[0][1][:, planes, :], diff[:], excess[:], larger0[:, planes, :], smaller0[:, planes, :]
-            )
-        diff1 = shared("diff1", [P, PACK, GROUP], F32, "excess0_1")
-        excess1 = sb("excess1", [P, PACK, GROUP], F32)
-        pair1 = shared("pair1", [P, 2, PACK, GROUP], F32, "pair1")
-        larger_smaller(early[1][0][:], early[1][1][:], diff1[:], excess1[:], pair1[:, 0], pair1[:, 1])
-
-        mean = [sb("mean%d" % c, [P, CHUNK, PACK], BF16) for c in range(CHUNKS)]
+        mean = [own("mean%d" % c, [P, CHUNK, PACK], BF16) for c in range(CHUNKS)]
 
         def make_mean(c, source, turned):
             for t in range(PACK):
@@ -175,10 +191,10 @@ def tile_picked_wpna_none_l_kernel(
                             is_transpose=True,
                         )
             for pair in range(BLOCKS // 2):
-                back = banks[4 + 2 * c + pair]
+                back = banks[BLOCKS + 2 * c + pair]
                 back_view = back[:].rearrange("p (u v) -> p u v", u=2)
-                for e in range(2):
-                    b = 2 * pair + e
+                for side in range(2):
+                    b = 2 * pair + side
                     nc.scalar.activation(
                         out=turned[b].rearrange("v (u p e) -> v u p e", u=2, e=2),
                         in_=banks[b][:].rearrange("v (u e p) -> v u p e", u=2, e=2),
@@ -187,79 +203,82 @@ def tile_picked_wpna_none_l_kernel(
                     )
                     words = turned[b].bitcast(F32)
                     for u in range(2):
-                        nc.tensor.transpose(back_view[:, u, e * P : (e + 1) * P], words[:, u * P : (u + 1) * P], identity[:])
+                        nc.tensor.transpose(
+                            back_view[:, u, side * P : (side + 1) * P], words[:, u * P : (u + 1) * P], identity[:]
+                        )
                 dst = mean[c][:, pair * 2 * P : (pair + 1) * 2 * P, :].rearrange("p v t -> p (v t)").bitcast(F32)
                 nc.scalar.copy(out=dst.rearrange("p (v u) -> p v u", u=2), in_=back[:].rearrange("p (u v) -> p v u", u=2))
 
-        def round_planes(dst, src):
-            nc.scalar.activation(out=dst.rearrange("p (v t) -> p v t", t=PACK), in_=src.rearrange("p t v -> p v t"), func=COPY)
+        def round_and_weave(dst, src):
+            nc.scalar.activation(
+                out=dst.rearrange("p (v t) -> p v t", t=PACK), in_=src.rearrange("p t v -> p v t"), func=COPY
+            )
 
-        W = CHUNK * PACK
-        two0 = sb("two0", [P, 2, CHUNK, PACK], BF16)
-
+        two0 = own("two0", [P, 2, CHUNK, PACK], BF16)
         for s, src in enumerate((larger0, smaller0)):
-            nc.scalar.activation(out=two0[:, s, :GROUP, :], in_=src[:].rearrange("p t v -> p v t"), func=COPY)
-        rounded_third0 = shared("rounded_third0", [P, W], BF16, "larger0")
-        round_planes(rounded_third0[:], third0[:])
-        turned0 = shared("turned0", [P, W], BF16, "smaller0")
+            nc.scalar.activation(out=two0[:, s, :GROUP, :], in_=src[:].rearrange("p (t v) -> p v t", t=PACK), func=COPY)
+        rounded_third0 = shared("rounded_third0", [P, WOVEN], BF16, "larger0")
+        round_and_weave(rounded_third0[:], third0[:])
+        turned0 = shared("turned0", [P, BLOCKS * H], BF16, "smaller0")
 
         def source0(d, t, b):
             if d == 2:
                 return third0[:, t, b * P : (b + 1) * P]
+            if t == 0:
+                return plane0[d][:, b * P : (b + 1) * P]
             g, inner = divmod(b * P, GROUP)
-            return early[g][d][:, t, inner : inner + P]
+            lo = (t - 1) * GROUP + inner
+            return rest[g][d][:, lo : lo + P]
 
         make_mean(0, source0, [turned0[:, b * H : (b + 1) * H] for b in range(BLOCKS)])
-        nc.scalar.activation(out=two0[:, :, GROUP:, :], in_=pair1[:].rearrange("p s t v -> p s v t"), func=COPY)
+        nc.scalar.activation(
+            out=two0[:, :, GROUP:, :], in_=both1[:].rearrange("p (s t v) -> p s v t", s=2, t=PACK), func=COPY
+        )
         third1 = shared("third1", [P, PACK, CHUNK], F32, "smaller0")
         for t in range(PACK):
             gather(third1[:, t, :], t, 2, CHUNK, T, PACK)
-        late.append(third1)
-        rounded1 = shared("rounded1", [P, 3 * W], BF16, "pair1")
+        picked1.append(third1)
+        rounded1 = shared("rounded1", [P, 3 * WOVEN], BF16, "both1")
+        two1 = own("two1", [P, 2, CHUNK, PACK], BF16)
         for d in range(3):
-            round_planes(rounded1[:, d * W : (d + 1) * W], late[d][:])
-        turned1 = [sb("turned1_%d" % b, [P, H], BF16) for b in range(BLOCKS)]
-        make_mean(1, lambda d, t, b: late[d][:, t, b * P : (b + 1) * P], [x[:] for x in turned1])
+            round_and_weave(rounded1[:, d * WOVEN : (d + 1) * WOVEN], picked1[d][:])
+        turned1 = [own("turned1_%d" % b, [P, H], BF16) for b in range(BLOCKS)]
+        make_mean(1, lambda d, t, b: picked1[d][:, t, b * P : (b + 1) * P], [tile[:] for tile in turned1])
 
         pieces = [[(0, CHUNK, banks[3])], [(0, CHUNK // 2, banks[7]), (CHUNK // 2, CHUNK, banks[3])]]
-        for c in range(CHUNKS):
+        for c, (two, third) in enumerate(((two0, rounded_third0[:]), (two1, rounded1[:, 2 * WOVEN :]))):
+            of_two = [two[:, s].rearrange("p v t -> p (v t)") for s in range(2)]
+            if c == 1:
+                for dst, op in zip(of_two, (MAX, MIN)):
+                    nc.vector.tensor_tensor(dst, rounded1[:, :WOVEN], rounded1[:, WOVEN : 2 * WOVEN], op)
             stats = []
-            if c == 0:
-                first = [two0[:, s].rearrange("p v t -> p (v t)") for s in range(2)]
-                last = rounded_third0[:]
-            else:
-                first = []
-                last = rounded1[:, 2 * W :]
-                for name, op in (("max", MAX), ("min", MIN)):
-                    two = sb("%s2_%d" % (name, c), [P, W], BF16)
-                    nc.vector.tensor_tensor(two[:], rounded1[:, :W], rounded1[:, W : 2 * W], op)
-                    first.append(two[:])
-            for (name, op), two in zip((("max", MAX), ("min", MIN)), first):
-                three = sb("%s3_%d" % (name, c), [P, W], BF16)
-                nc.vector.tensor_tensor(three[:], two, last, op)
-                stats.append(three[:])
+            for s, op in enumerate((MAX, MIN)):
+                of_three = own("of_three%d_%d" % (c, s), [P, WOVEN], BF16)
+                nc.vector.tensor_tensor(of_three[:], of_two[s], third, op)
+                stats.append(of_three[:])
             stats.append(mean[c][:].rearrange("p v t -> p (v t)"))
-            for s in range(3):
-                codes = sb("z_codes%d_%d" % (c, s), [P, CHUNK], U32)
-                plane = sb("z_plane%d_%d" % (c, s), [P, CHUNK], U8)
-                spans = [(lo, hi) for lo, hi, bank in pieces[c]] if s == 2 else [(0, CHUNK)]
+            for s, stat in enumerate(stats):
+                last_pass = s == len(stats) - 1
+                codes = own("z_codes%d_%d" % (c, s), [P, CHUNK], U32)
+                scale_tile = own("z_scale_tile%d_%d" % (c, s), [P, CHUNK], U8)
+                spans = [(lo, hi) for lo, hi, bank in pieces[c]] if last_pass else [(0, CHUNK)]
                 for lo, hi in spans:
                     nc.vector.quantize_mx(
-                        out=codes[:, lo:hi].bitcast(FP8X4), scales=plane[:, lo:hi], in_=stats[s][:, lo * PACK : hi * PACK]
+                        out=codes[:, lo:hi].bitcast(FP8X4), scales=scale_tile[:, lo:hi], in_=stat[:, lo * PACK : hi * PACK]
                     )
                 for lo, hi, bank in pieces[c]:
                     nc.tensor.matmul_mx(
                         out=bank[:, : hi - lo],
                         lhsT=wz_codes[s][:].bitcast(FP8X4),
-                        lhsT_scale=wz_planes[s][:],
+                        lhsT_scale=wz_scale_tiles[s][:],
                         rhs=codes[:, lo:hi].bitcast(FP8X4),
-                        rhs_scale=plane[:, lo:hi],
+                        rhs_scale=scale_tile[:, lo:hi],
                         start=(s == 0),
-                        stop=(s == 2),
+                        stop=last_pass,
                     )
             for i, (lo, hi, bank) in enumerate(pieces[c]):
-                result = sb("result%d_%d" % (c, i), [P, hi - lo], F32)
-                if (c, i) == (CHUNKS - 1, 1):
+                result = own("result%d_%d" % (c, i), [P, hi - lo], F32)
+                if c * CHUNK + hi == T:
                     nc.vector.tensor_copy(out=result[:], in_=bank[:, : hi - lo])
                 else:
                     nc.scalar.copy(out=result[:], in_=bank[:, : hi - lo])

from contextlib import ExitStack

import concourse.mybir as mybir
from concourse.masks import make_identity

K, T, H, N = 512, 1024, 512, 128
FLOPS = 2 * K * H * T + 3 * 2 * H * N * T

F32 = mybir.dt.float32
BF16 = mybir.dt.bfloat16
I32 = mybir.dt.int32
U32 = mybir.dt.uint32
U16 = mybir.dt.uint16
U8 = mybir.dt.uint8
FP8X4 = mybir.dt.float8_e4m3fn_x4
MAX = mybir.AluOpType.max
MIN = mybir.AluOpType.min
ADD = mybir.AluOpType.add
SUB = mybir.AluOpType.subtract
COPY = mybir.ActivationFunctionType.Copy
F32_MAX = 3.4028234663852886e38

P = 128
PACK = 4
BANK = 512
CHUNK = 512
CHUNKS = T // CHUNK
BLOCKS = CHUNK // P
GROUP = CHUNK // 2
WOVEN = CHUNK * PACK
PER_COLUMN = 16


def tile_picked_wpna_none_l_kernel(
    tc, x_words, x_scales, w1, w2_words, w2_scales, w3_words, w3_scales, w4_words, w4_scales, pos1, pos2, pos3, out
):
    nc = tc.nc
    with ExitStack() as ctx:
        keep = ctx.enter_context(tc.tile_pool(name="keep", bufs=1))
        psum = ctx.enter_context(tc.psum_pool(name="psum", bufs=1))

        def own(name, shape, dtype):
            return keep.tile(shape, dtype, name=name, align_bytes=64)

        def shared(name, shape, dtype, tag):
            return keep.tile(shape, dtype, name=name, tag=tag, align_bytes=64)

        banks = [psum.tile([P, BANK], F32, name="bank%d" % b) for b in range(8)]

        def load_scale_rows(queue, scale_tile, rows):
            for q in range(4):
                queue.dma_start(
                    out=scale_tile[32 * q : 32 * q + 4, :].bitcast(I32), in_=rows[4 * q : 4 * q + 4, :].bitcast(I32)
                )

        x_scale_tile = own("x_scale_tile", [P, T], U8)
        nc.gpsimd.memset(x_scale_tile[:].bitcast(I32), 0)
        w1_rows = w1.rearrange("(p j) c -> p j c", j=PACK)
        half_h = H // 2
        w1_raw = []
        for a in range(2):
            raw = own("w1_raw%d" % a, [P, PACK, half_h], F32)
            nc.sync.dma_start(out=raw[:], in_=w1_rows[:, :, a * half_h : (a + 1) * half_h])
            w1_raw.append(raw)
        load_scale_rows(nc.scalar, x_scale_tile, x_scales[0])
        x_flat = x_words[0].rearrange("p c r -> p (c r)")
        x_codes = []
        for u in range(T // BANK):
            codes = own("x_codes%d" % u, [P, BANK], U32)
            nc.sync.dma_start(out=codes[:].bitcast(I32), in_=x_flat[:, u * BANK * PACK : (u + 1) * BANK * PACK].bitcast(I32))
            x_codes.append(codes)
        lists = []
        for d, pos in enumerate((pos1, pos2, pos3)):
            offsets = keep.tile([P, T // PER_COLUMN], U16, name="list%d" % d)
            nc.sync.dma_start(offsets[:], pos)
            lists.append(offsets)
        wz_codes, wz_scale_tiles = [], []
        for s, (words, scales) in enumerate(((w3_words, w3_scales), (w4_words, w4_scales), (w2_words, w2_scales))):
            codes = own("wz_codes%d" % s, [P, N], U32)
            nc.sync.dma_start(out=codes[:].bitcast(I32), in_=words[0].rearrange("p c r -> p (c r)").bitcast(I32))
            scale_tile = own("wz_scale_tile%d" % s, [P, N], U8)
            nc.gpsimd.memset(scale_tile[:].bitcast(I32), 0)
            load_scale_rows(nc.sync, scale_tile, scales[0])
            wz_codes.append(codes)
            wz_scale_tiles.append(scale_tile)
        identity = own("identity", [P, P], F32)
        make_identity(nc, identity[:])

        sets = ((0, 1), (1, 2), (2, 4))
        w1_bf = [own("w1_bf%d" % lo, [P, hi - lo, P, PACK], BF16) for lo, hi in sets]
        w1_codes = [own("w1_codes%d" % lo, [P, (hi - lo) * P], U32) for lo, hi in sets]
        w1_scale_tiles = [own("w1_scale_tile%d" % lo, [P, (hi - lo) * P], U8) for lo, hi in sets]
        half_m = P // 2
        dealt = [raw[:].rearrange("p j (m t) -> p t m j", t=PACK) for raw in w1_raw]

        def w1_part(s, a, lo, hi):
            return w1_bf[s][:, :, a * half_m + lo : a * half_m + hi, :], dealt[a][:, sets[s][0] : sets[s][1], lo:hi, :]

        nc.vector.tensor_copy(*w1_part(0, 0, 0, half_m))
        nc.vector.tensor_copy(*w1_part(1, 0, 0, half_m))
        nc.scalar.activation(*w1_part(2, 0, 0, half_m), func=COPY)
        nc.vector.tensor_copy(*w1_part(0, 1, 0, half_m // 2))
        nc.scalar.activation(*w1_part(0, 1, half_m // 2, half_m), func=COPY)
        nc.scalar.activation(*w1_part(1, 1, 0, half_m), func=COPY)
        nc.scalar.activation(*w1_part(2, 1, 0, half_m), func=COPY)
        for s in range(len(sets)):
            nc.vector.quantize_mx(
                out=w1_codes[s][:].bitcast(FP8X4),
                scales=w1_scale_tiles[s][:],
                in_=w1_bf[s][:].rearrange("p t m j -> p (t m j)"),
            )

        h = own("h", [P, PACK * T], F32)
        for t in range(PACK):
            s = min(t, len(sets) - 1)
            m_cols = slice((t - s) * P, (t - s + 1) * P)
            width = BANK // 2 if t == 0 else BANK
            for i, lo in enumerate(range(0, T, width)):
                bank = banks[i if t == 0 else 2 * (t - 1) + i]
                u, inner = divmod(lo, BANK)
                nc.tensor.matmul_mx(
                    out=bank[:, :width],
                    lhsT=w1_codes[s][:, m_cols].bitcast(FP8X4),
                    lhsT_scale=w1_scale_tiles[s][:, m_cols],
                    rhs=x_codes[u][:, inner : inner + width].bitcast(FP8X4),
                    rhs_scale=x_scale_tile[:, lo : lo + width],
                    start=True,
                    stop=True,
                )
                dst = h[:, t * T + lo : t * T + lo + width]
                if t == 0 and i % 2 == 1:
                    nc.vector.tensor_copy(out=dst, in_=bank[:, :width])
                else:
                    nc.scalar.copy(out=dst, in_=bank[:, :width])

        def gather(dst, t, d, lo, hi, span):
            end = min(t + span, PACK) * T
            offsets = lists[d][:, lo // PER_COLUMN : hi // PER_COLUMN]
            nc.vector.tensor_copy(out=dst, in_=h[:, t * T : end].indirect(offsets))

        plane0 = [own("plane0_%d" % d, [P, CHUNK], F32) for d in range(2)]
        rest = [[own("rest%d_%d" % (g, d), [P, (PACK - 1) * GROUP], F32) for d in range(2)] for g in range(2)]
        for d in range(2):
            gather(plane0[d][:], 0, d, 0, CHUNK, 1)
        for g in range(2):
            for t in range(1, PACK):
                for d in range(2):
                    gather(rest[g][d][:, (t - 1) * GROUP : t * GROUP], t, d, g * GROUP, (g + 1) * GROUP, 1 + g)
        third0 = own("third0", [P, PACK, CHUNK], F32)
        for t in range(PACK):
            gather(third0[:, t, :], t, 2, 0, CHUNK, PACK)
        picked1 = [own("picked1_%d" % d, [P, PACK, CHUNK], F32) for d in range(2)]
        for d in range(2):
            for t in range(PACK):
                gather(picked1[d][:, t, :], t, d, CHUNK, T, PACK)

        group_cols = PACK * GROUP
        larger0 = shared("larger0", [P, group_cols], F32, "larger0")
        smaller0 = shared("smaller0", [P, group_cols], F32, "smaller0")
        both1 = shared("both1", [P, 2 * group_cols], F32, "both1")
        extremes = ((larger0[:], smaller0[:]), (both1[:, :group_cols], both1[:, group_cols:]))
        diff = own("diff_plane0", [P, CHUNK], F32)
        excess = shared("excess_plane0", [P, CHUNK], F32, "excess0")
        nc.gpsimd.tensor_tensor(diff[:], plane0[0][:], plane0[1][:], SUB)
        nc.gpsimd.tensor_scalar(excess[:], diff[:], F32_MAX, 0.0, MIN, MAX)
        for g, (larger, smaller) in enumerate(extremes):
            cols = slice(g * GROUP, (g + 1) * GROUP)
            nc.gpsimd.tensor_tensor(larger[:, :GROUP], plane0[1][:, cols], excess[:, cols], ADD)
            nc.gpsimd.tensor_tensor(smaller[:, :GROUP], plane0[0][:, cols], excess[:, cols], SUB)
        for g, (larger, smaller) in enumerate(extremes):
            a, b = rest[g]
            diff = shared("diff_rest%d" % g, [P, group_cols - GROUP], F32, "excess%d" % g)
            excess = shared("excess_rest%d" % g, [P, group_cols - GROUP], F32, "excess%d" % (g + 1))
            nc.gpsimd.tensor_tensor(diff[:], a[:], b[:], SUB)
            nc.gpsimd.tensor_scalar(excess[:], diff[:], F32_MAX, 0.0, MIN, MAX)
            nc.gpsimd.tensor_tensor(larger[:, GROUP:], b[:], excess[:], ADD)
            nc.gpsimd.tensor_tensor(smaller[:, GROUP:], a[:], excess[:], SUB)

        mean = [own("mean%d" % c, [P, CHUNK, PACK], BF16) for c in range(CHUNKS)]

        def make_mean(c, source, turned):
            for t in range(PACK):
                for b in range(BLOCKS):
                    for d in (2, 1, 0):
                        nc.tensor.matmul(
                            banks[b][:, t * P : (t + 1) * P],
                            source(d, t, b),
                            identity[:],
                            start=(d == 2),
                            stop=(d == 0),
                            is_transpose=True,
                        )
            for pair in range(BLOCKS // 2):
                back = banks[BLOCKS + 2 * c + pair]
                back_view = back[:].rearrange("p (u v) -> p u v", u=2)
                for side in range(2):
                    b = 2 * pair + side
                    nc.scalar.activation(
                        out=turned[b].rearrange("v (u p e) -> v u p e", u=2, e=2),
                        in_=banks[b][:].rearrange("v (u e p) -> v u p e", u=2, e=2),
                        func=COPY,
                        scale=1.0 / 3.0,
                    )
                    words = turned[b].bitcast(F32)
                    for u in range(2):
                        nc.tensor.transpose(
                            back_view[:, u, side * P : (side + 1) * P], words[:, u * P : (u + 1) * P], identity[:]
                        )
                dst = mean[c][:, pair * 2 * P : (pair + 1) * 2 * P, :].rearrange("p v t -> p (v t)").bitcast(F32)
                nc.scalar.copy(out=dst.rearrange("p (v u) -> p v u", u=2), in_=back[:].rearrange("p (u v) -> p v u", u=2))

        def round_and_weave(dst, src):
            nc.scalar.activation(
                out=dst.rearrange("p (v t) -> p v t", t=PACK), in_=src.rearrange("p t v -> p v t"), func=COPY
            )

        two0 = own("two0", [P, 2, CHUNK, PACK], BF16)
        for s, src in enumerate((larger0, smaller0)):
            nc.scalar.activation(out=two0[:, s, :GROUP, :], in_=src[:].rearrange("p (t v) -> p v t", t=PACK), func=COPY)
        rounded_third0 = shared("rounded_third0", [P, WOVEN], BF16, "larger0")
        round_and_weave(rounded_third0[:], third0[:])
        turned0 = shared("turned0", [P, BLOCKS * H], BF16, "smaller0")

        def source0(d, t, b):
            if d == 2:
                return third0[:, t, b * P : (b + 1) * P]
            if t == 0:
                return plane0[d][:, b * P : (b + 1) * P]
            g, inner = divmod(b * P, GROUP)
            lo = (t - 1) * GROUP + inner
            return rest[g][d][:, lo : lo + P]

        make_mean(0, source0, [turned0[:, b * H : (b + 1) * H] for b in range(BLOCKS)])
        nc.scalar.activation(
            out=two0[:, :, GROUP:, :], in_=both1[:].rearrange("p (s t v) -> p s v t", s=2, t=PACK), func=COPY
        )
        third1 = shared("third1", [P, PACK, CHUNK], F32, "smaller0")
        for t in range(PACK):
            gather(third1[:, t, :], t, 2, CHUNK, T, PACK)
        picked1.append(third1)
        rounded1 = shared("rounded1", [P, 3 * WOVEN], BF16, "both1")
        two1 = own("two1", [P, 2, CHUNK, PACK], BF16)
        for d in range(3):
            round_and_weave(rounded1[:, d * WOVEN : (d + 1) * WOVEN], picked1[d][:])
        turned1 = [own("turned1_%d" % b, [P, H], BF16) for b in range(BLOCKS)]
        make_mean(1, lambda d, t, b: picked1[d][:, t, b * P : (b + 1) * P], [tile[:] for tile in turned1])

        pieces = [[(0, CHUNK, banks[3])], [(0, CHUNK // 2, banks[7]), (CHUNK // 2, CHUNK, banks[3])]]
        for c, (two, third) in enumerate(((two0, rounded_third0[:]), (two1, rounded1[:, 2 * WOVEN :]))):
            of_two = [two[:, s].rearrange("p v t -> p (v t)") for s in range(2)]
            if c == 1:
                for dst, op in zip(of_two, (MAX, MIN)):
                    nc.vector.tensor_tensor(dst, rounded1[:, :WOVEN], rounded1[:, WOVEN : 2 * WOVEN], op)
            stats = []
            for s, op in enumerate((MAX, MIN)):
                of_three = own("of_three%d_%d" % (c, s), [P, WOVEN], BF16)
                nc.vector.tensor_tensor(of_three[:], of_two[s], third, op)
                stats.append(of_three[:])
            stats.append(mean[c][:].rearrange("p v t -> p (v t)"))
            for s, stat in enumerate(stats):
                last_pass = s == len(stats) - 1
                codes = own("z_codes%d_%d" % (c, s), [P, CHUNK], U32)
                scale_tile = own("z_scale_tile%d_%d" % (c, s), [P, CHUNK], U8)
                spans = [(lo, hi) for lo, hi, bank in pieces[c]] if last_pass else [(0, CHUNK)]
                for lo, hi in spans:
                    nc.vector.quantize_mx(
                        out=codes[:, lo:hi].bitcast(FP8X4), scales=scale_tile[:, lo:hi], in_=stat[:, lo * PACK : hi * PACK]
                    )
                for lo, hi, bank in pieces[c]:
                    nc.tensor.matmul_mx(
                        out=bank[:, : hi - lo],
                        lhsT=wz_codes[s][:].bitcast(FP8X4),
                        lhsT_scale=wz_scale_tiles[s][:],
                        rhs=codes[:, lo:hi].bitcast(FP8X4),
                        rhs_scale=scale_tile[:, lo:hi],
                        start=(s == 0),
                        stop=last_pass,
                    )
            for i, (lo, hi, bank) in enumerate(pieces[c]):
                result = own("result%d_%d" % (c, i), [P, hi - lo], F32)
                if c * CHUNK + hi == T:
                    nc.vector.tensor_copy(out=result[:], in_=bank[:, : hi - lo])
                else:
                    nc.scalar.copy(out=result[:], in_=bank[:, : hi - lo])
                nc.sync.dma_start(out=out[:, c * CHUNK + lo : c * CHUNK + hi], in_=result[:])
